import numpy as np
import ml_dtypes


def mxq(x, axis, fmt="e4m3"):
    dtype, down = {"e4m3": (ml_dtypes.float8_e4m3fn, 7), "e5m2": (ml_dtypes.float8_e5m2, 14)}[fmt]
    v = np.moveaxis(np.asarray(x, np.float32).astype(ml_dtypes.bfloat16).astype(np.float64), axis, -1)
    blocks = v.reshape(v.shape[:-1] + (-1, 32))
    amax = np.abs(blocks).max(-1, keepdims=True)
    byte = np.maximum(np.where(amax > 0, np.frexp(amax)[1] - 1 + 127, 0) - down, 1)
    scale = np.exp2(byte - 127.0)
    codes = (blocks / scale).astype(np.float32).astype(dtype).astype(np.float64)
    return np.moveaxis((codes * scale).reshape(v.shape), -1, axis)


WIDE = False


def mx_kscale(k):
    if not WIDE:
        return np.ones(k)
    levels = np.array([10, -10, 5, -5, 0])
    if k % 512:
        return np.exp2(np.random.permutation(np.resize(levels, k // 32))).repeat(32)
    a = np.empty((k // 512, 16))
    for p in range(k // 512):
        a[p, :8] = np.random.permutation(np.resize(levels, 8))
        for g in range(8):
            far = levels[np.abs(levels - a[p, g]) >= 10]
            a[p, g + 8] = far[np.random.randint(len(far))]
    return np.exp2(a.ravel()).repeat(32)


def f64(x):
    return np.asarray(x).astype(np.float64)


def striped(idx):
    return np.tile(idx.reshape(-1, 16).T, (8, 1)).astype(np.uint16)


def unstriped(offs):
    return offs[:16].T.reshape(-1).astype(np.int64)


E2M1 = np.array([0.0, 0.5, 1.0, 1.5, 2.0, 3.0, 4.0, 6.0, -0.0, -0.5, -1.0, -1.5, -2.0, -3.0, -4.0, -6.0])


def pack_weight(w, fmt):
    k, n = w.shape
    w = f64(np.asarray(w, np.float32).astype(ml_dtypes.bfloat16)).reshape(k // 32, 32, n)
    amax = np.abs(w).max(1)
    if fmt == "e4m3":
        byte = np.frexp(amax)[1] - 1 + 127 - 7
    else:
        mant, ex = np.frexp(amax / 6.0)
        byte = np.where(mant > 0.5, ex, ex - 1) + 127
    byte = np.clip(np.where(amax > 0, byte, 1), 1, 254)
    scaled = (w * np.exp2(127.0 - byte)[:, None, :]).reshape(k, n).astype(np.float32)
    by_word = np.ascontiguousarray(scaled.reshape(k // 512, 128, 4, n).transpose(0, 1, 3, 2))
    if fmt == "e4m3":
        words = by_word.astype(ml_dtypes.float8_e4m3fn).view(np.uint8)
    else:
        c = by_word.astype(ml_dtypes.float4_e2m1fn).view(np.uint8) & 0xF
        words = (c[..., 0::2] | (c[..., 1::2] << 4)).reshape(k // 512, 128, 2 * n)
    return np.ascontiguousarray(words), np.ascontiguousarray(byte.astype(np.uint8).reshape(k // 512, 16, n))


def unpack_weight(words, scales, fmt):
    g, _, n = scales.shape
    words = np.ascontiguousarray(words).reshape(g, 128, n, -1)
    if fmt == "e4m3":
        vals = words.view(ml_dtypes.float8_e4m3fn).astype(np.float64)
    else:
        nib = np.empty((g, 128, n, 4), np.uint8)
        nib[..., 0::2] = words & 0xF
        nib[..., 1::2] = words >> 4
        vals = E2M1[nib]
    vals = vals * np.repeat(np.exp2(scales.astype(np.float64) - 127.0), 8, axis=1)[..., None]
    return vals.transpose(0, 1, 3, 2).reshape(g * 512, n)


def gelu(v):
    return 0.5 * v * (1.0 + np.tanh(np.sqrt(2.0 / np.pi) * (v + 0.044715 * v**3)))


K, H, N, T, T2, S = 512, 1024, 256, 2048, 2048, 1024


def setup_inputs():
    n = np.random.standard_normal
    s = mx_kscale(K)[:, None]
    u = mx_kscale(H)[:, None]
    tab_words, tab_scales = pack_weight(n((K, T)) * s, "e4m3")
    wa_words, wa_scales = pack_weight(n((K, H)) / np.sqrt(K) / s * u.T, "e2m1")
    wk_words, wk_scales = pack_weight(n((H, N)) / np.sqrt(H) / u, "e4m3")
    return {
        "tab_words": tab_words, "tab_scales": tab_scales,
        "offs": striped(np.random.permutation(T)[:S]),
        "xT": (np.round(16 * n((K, T2))) / 16).astype(np.float32),
        "offs2": striped(np.random.permutation(T2)[:S]),
        "offs3": striped(np.random.permutation(T2)[:S]),
        "pw": (np.exp2(np.random.randint(-1, 2, K)) * s[:, 0]).astype(np.float32),
        "wa_words": wa_words, "wa_scales": wa_scales,
        "wg": (n((K, H)) / np.sqrt(K) / s).astype(np.float32),
        "bg": (0.5 * n(H)).astype(np.float32),
        "wx": (n((K, H)) / np.sqrt(K) / s * u.T).astype(np.float32),
        "wo": (n((H, N)) / np.sqrt(H) / u).astype(np.float32),
        "wk_words": wk_words, "wk_scales": wk_scales,
    }


def reference(tab_words, tab_scales, offs, xT, offs2, offs3, pw,
              wa_words, wa_scales, wg, bg, wx, wo, wk_words, wk_scales):
    v = unpack_weight(tab_words, tab_scales, "e4m3")[:, unstriped(offs)]
    wa = unpack_weight(wa_words, wa_scales, "e2m1")
    wk = unpack_weight(wk_words, wk_scales, "e4m3")
    x = f64(xT)[:, unstriped(offs2)] * f64(xT)[:, unstriped(offs3)]
    x = x * f64(pw)[:, None]
    a = np.maximum(wa.T @ v, 0)
    c = (mxq(f64(wg), 0, "e4m3").T @ v) + f64(bg)[:, None]
    b = mxq(f64(wx), 0, "e4m3").T @ mxq(x, 0, "e4m3")
    z = b * (1 / (1 + np.exp(-c)))
    y = mxq(f64(wo), 0, "e4m3").T @ mxq(z, 0, "e4m3") + wk.T @ mxq(a, 0, "e4m3")
    return y

@@ -1,0 +1,231 @@
+from contextlib import ExitStack
+
+import concourse.mybir as mybir
+
+K, H, N, T, S = 512, 1024, 256, 2048, 1024
+FLOPS = 2 * S * (3 * K * H + 2 * H * N)
+
+F32 = mybir.dt.float32
+BF16 = mybir.dt.bfloat16
+I32 = mybir.dt.int32
+U32 = mybir.dt.uint32
+U16 = mybir.dt.uint16
+U8 = mybir.dt.uint8
+FP8X4 = mybir.dt.float8_e4m3fn_x4
+FP4X4 = mybir.dt.float4_e2m1fn_x4
+ACT = mybir.ActivationFunctionType
+MULT = mybir.AluOpType.mult
+
+P = 128
+PACK = 4
+PASS = P * PACK
+R_PASSES = H // PASS
+HALF = 512
+HALVES = S // HALF
+CHUNK = 256
+CHUNKS = S // CHUNK
+LIST_COLS = HALF // 16
+
+
+def tile_list_aerosol_activation_features_kernel(
+    tc, tab_words, tab_scales, offs, xT, offs2, offs3, pw, wa_words, wa_scales, wg, bg, wx, wo, wk_words, wk_scales, out
+):
+    nc = tc.nc
+    with ExitStack() as ctx:
+        keep = ctx.enter_context(tc.tile_pool(name="keep", bufs=1))
+        ring = ctx.enter_context(tc.tile_pool(name="ring", bufs=2))
+        psum = ctx.enter_context(tc.psum_pool(name="psum", bufs=2))
+
+        def held(shape, dtype, name):
+            return keep.tile(shape, dtype, name=name, align_bytes=64)
+
+        def mx_tiles(width, name):
+            return held([P, width], U32, name + "_codes"), held([P, width], U8, name + "_scales")
+
+        def quantize(codes, scales, values):
+            nc.vector.quantize_mx(out=codes[:].bitcast(FP8X4), scales=scales[:], in_=values)
+
+        def mm(acc, lhs, lhs_cols, rhs, rhs_cols, start=True, stop=True):
+            nc.tensor.matmul_mx(
+                out=acc,
+                lhsT=lhs[0][:, lhs_cols].bitcast(FP8X4),
+                lhsT_scale=lhs[1][:, lhs_cols],
+                rhs=rhs[0][:, rhs_cols].bitcast(FP8X4),
+                rhs_scale=rhs[1][:, rhs_cols],
+                start=start,
+                stop=stop,
+            )
+
+        list1 = held([P, S // 16], U16, "list1")
+        list2 = held([P, S // 16], U16, "list2")
+        list3 = held([P, S // 16], U16, "list3")
+        tab_w = held([P, T], I32, "tab_w")
+        tab_s = held([P, T], U8, "tab_s")
+        wa_raw_w = held([P, 2 * H], U8, "wa_raw_w")
+        wa_raw_s = held([P, H], U8, "wa_raw_s")
+        wk_w = held([P, R_PASSES * N], I32, "wk_w")
+        wk_s = held([P, R_PASSES * N], U8, "wk_s")
+        pw_sb = held([P, PACK], F32, "pw_sb")
+        bg_sb = held([P, R_PASSES, PACK], F32, "bg_sb")
+        planes = [held([P, T], F32, "plane%d" % i) for i in range(PACK)]
+        wg_raw = [held([P, PACK, PASS], F32, "wg_raw%d" % a) for a in range(R_PASSES)]
+        wx_raw = [held([P, PACK, PASS], F32, "wx_raw%d" % a) for a in range(R_PASSES)]
+        wo_raw = held([P, R_PASSES, PACK, N], F32, "wo_raw")
+        warm = held([P, 2], F32, "warm")
+
+        for plane in (tab_s, wa_raw_s, wk_s):
+            nc.gpsimd.memset(plane[:].bitcast(I32), 0)
+        nc.vector.memset(warm[:, 0:1], 0.0)
+        nc.scalar.activation(warm[:, 1:2], warm[:, 0:1], ACT.Sigmoid)
+
+        x_rows = xT.rearrange("(p i) t -> p i t", i=PACK)
+        wg_rows = wg.rearrange("(p i) r -> p i r", i=PACK)
+        wx_rows = wx.rearrange("(p i) r -> p i r", i=PACK)
+
+        nc.sync.dma_start(list1[:], offs)
+        nc.sync.dma_start(list3[:], offs3)
+        nc.sync.dma_start(list2[:], offs2)
+        for q in range(4):
+            nc.scalar.dma_start(tab_s[32 * q : 32 * q + 4, :].bitcast(I32), tab_scales[0, 4 * q : 4 * q + 4, :].bitcast(I32))
+        nc.sync.dma_start(tab_w[:], tab_words[0].rearrange("p t i -> p (t i)").bitcast(I32))
+        nc.sync.dma_start(wa_raw_w[:].bitcast(I32), wa_words[0].bitcast(I32))
+        for q in range(4):
+            nc.scalar.dma_start(wa_raw_s[32 * q : 32 * q + 4, :].bitcast(I32), wa_scales[0, 4 * q : 4 * q + 4, :].bitcast(I32))
+        nc.scalar.dma_start(pw_sb[:], pw.rearrange("(p i) -> p i", i=PACK))
+        nc.scalar.dma_start(bg_sb[:], bg.rearrange("(a p i) -> p a i", p=P, i=PACK))
+        weight_loads = [(wg_raw[a], wg_rows, a) for a in range(R_PASSES)] + [(wx_raw[a], wx_rows, a) for a in range(R_PASSES)]
+        for i in range(PACK):
+            nc.sync.dma_start(planes[i][:], x_rows[:, i, :])
+            raw, rows, a = weight_loads[i]
+            nc.sync.dma_start(raw[:], rows[:, :, a * PASS : (a + 1) * PASS])
+        nc.sync.dma_start(
+            wo_raw[:].rearrange("p a i n -> p a (i n)"), wo.rearrange("(a p i) n -> p a (i n)", p=P, i=PACK)
+        )
+        nc.sync.dma_start(
+            wk_w[:].rearrange("p (a n) -> p a n", a=R_PASSES),
+            wk_words.rearrange("a p n i -> p a (n i)").bitcast(I32),
+        )
+        for q in range(4):
+            nc.sync.dma_start(
+                wk_s[32 * q : 32 * q + 4, :].bitcast(I32).rearrange("r (a n) -> r a n", a=R_PASSES),
+                wk_scales[:, 4 * q : 4 * q + 4, :].bitcast(I32).rearrange("a r n -> r a n"),
+            )
+
+        def list_half(tile, h):
+            return tile[:, h * LIST_COLS : (h + 1) * LIST_COLS]
+
+        v = [mx_tiles(HALF, "v%d" % h) for h in range(HALVES)]
+        for h in range(HALVES):
+            nc.vector.tensor_copy(v[h][1][:], tab_s[:].indirect(list_half(list1, h)))
+        wa_w = held([P, 2 * H], U8, "wa_w")
+        wa_s = held([P, H], U8, "wa_s")
+        nc.vector.tensor_copy(v[0][0][:], tab_w[:].bitcast(U32).indirect(list_half(list1, 0)))
+        nc.vector.tensor_copy(
+            wa_w[:].bitcast(U16).rearrange("p (a t m) -> p a m t", a=R_PASSES, t=PACK),
+            wa_raw_w[:].bitcast(U16).rearrange("p (a m t) -> p a m t", a=R_PASSES, t=PACK),
+        )
+        nc.vector.tensor_copy(
+            wa_s[:].rearrange("p (a t m) -> p a m t", a=R_PASSES, t=PACK),
+            wa_raw_s[:].rearrange("p (a m t) -> p a m t", a=R_PASSES, t=PACK),
+        )
+        nc.vector.tensor_copy(v[1][0][:], tab_w[:].bitcast(U32).indirect(list_half(list1, 1)))
+
+        prod = [held([P, PACK, HALF], F32, "prod%d" % h) for h in range(HALVES)]
+        for i in range(PACK):
+            humid = []
+            for h in range(HALVES):
+                picked = ring.tile([P, HALF], F32, name="picked", bufs=4, align_bytes=64)
+                nc.vector.tensor_copy(picked[:], planes[i][:].indirect(list_half(list3, h)))
+                nc.scalar.activation(picked[:], picked[:], ACT.Copy, scale=pw_sb[:, i : i + 1])
+                humid.append(picked)
+            for h in range(HALVES):
+                nc.vector.tensor_tensor(prod[h][:, i, :], planes[i][:].indirect(list_half(list2, h)), humid[h][:], MULT)
+        xq = [mx_tiles(HALF, "x%d" % h) for h in range(HALVES)]
+        for h in range(HALVES):
+            x_bf = ring.tile([P, HALF * PACK], BF16, name="x_bf", align_bytes=64)
+            nc.vector.tensor_copy(
+                x_bf[:].rearrange("p (c e i) -> p c i e", e=4, i=PACK),
+                prod[h][:].rearrange("p i (c e) -> p c i e", e=4),
+            )
+            quantize(xq[h][0], xq[h][1], x_bf[:])
+
+        def first_stage_weight(raw, name):
+            w_bf = ring.tile([P, PASS * PACK], BF16, name="w_bf", align_bytes=64)
+            nc.scalar.copy(
+                w_bf[:].rearrange("p (u e m i) -> p u m i e", u=2, e=2, i=PACK),
+                raw[:].rearrange("p i (m u e) -> p u m i e", u=2, e=2),
+            )
+            tiles = mx_tiles(PASS, name)
+            quantize(tiles[0], tiles[1], w_bf[:])
+            return tiles
+
+        wgq = [first_stage_weight(wg_raw[a], "wg%d" % a) for a in range(R_PASSES)]
+        wxq = [first_stage_weight(wx_raw[a], "wx%d" % a) for a in range(R_PASSES)]
+        wo_bf = ring.tile([P, PASS * PACK], BF16, name="w_bf", align_bytes=64)
+        nc.scalar.copy(
+            wo_bf[:].rearrange("p (a c e i) -> p a c i e", a=R_PASSES, e=2, i=PACK),
+            wo_raw[:].rearrange("p a i (c e) -> p a c i e", e=2),
+        )
+        woq = mx_tiles(R_PASSES * N, "wo")
+        quantize(woq[0], woq[1], wo_bf[:])
+
+        gate = {}
+        for h in range(HALVES):
+            for a in range(R_PASSES):
+                gate[h, a] = held([P, PACK, HALF], F32, "gate%d%d" % (h, a))
+                for t in range(PACK):
+                    c_bank = psum.tile([P, HALF], F32, name="c_bank")
+                    mm(c_bank[:], wgq[a], slice(t * P, (t + 1) * P), v[h], slice(0, HALF))
+                    nc.scalar.activation(gate[h, a][:, t, :], c_bank[:], ACT.Sigmoid, bias=bg_sb[:, a, t : t + 1])
+
+        aq = [mx_tiles(R_PASSES * CHUNK, "a%d" % q) for q in range(CHUNKS)]
+        for q in range(CHUNKS):
+            h, first = divmod(q * CHUNK, HALF)
+            a_bf = ring.tile([P, R_PASSES, CHUNK, PACK], BF16, name="a_bf", bufs=3, align_bytes=64)
+            for a in range(R_PASSES):
+                for j0 in range(0, CHUNK, P):
+                    cols = slice(first + j0, first + j0 + P)
+                    a_bank = psum.tile([P, PACK, P], F32, name="a_bank")
+                    for t in range(PACK):
+                        r0 = a * PASS + t * P
+                        nc.tensor.matmul_mx(
+                            out=a_bank[:, t, :],
+                            lhsT=wa_w[:, 2 * r0 : 2 * (r0 + P)].bitcast(FP4X4),
+                            lhsT_scale=wa_s[:, r0 : r0 + P],
+                            rhs=v[h][0][:, cols].bitcast(FP8X4),
+                            rhs_scale=v[h][1][:, cols],
+                            start=True,
+                            stop=True,
+                        )
+                    nc.scalar.activation(a_bf[:, a, j0 : j0 + P, :], a_bank[:].rearrange("p t j -> p j t"), ACT.Relu)
+            quantize(aq[q][0], aq[q][1], a_bf[:].rearrange("p a j t -> p (a j t)"))
+
+        out_rows = out.rearrange("(u p) j -> p u j", p=P)
+        for q in range(CHUNKS):
+            h, first = divmod(q * CHUNK, HALF)
+            z_bf = ring.tile([P, R_PASSES, CHUNK, PACK], BF16, name="z_bf", align_bytes=64)
+            for a in range(R_PASSES):
+                for j0 in range(0, CHUNK, P):
+                    cols = slice(first + j0, first + j0 + P)
+                    b_bank = psum.tile([P, PACK, P], F32, name="b_bank", bufs=3)
+                    for t in range(PACK):
+                        mm(b_bank[:, t, :], wxq[a], slice(t * P, (t + 1) * P), xq[h], cols)
+                    nc.vector.tensor_tensor(
+                        z_bf[:, a, j0 : j0 + P, :].rearrange("p (c e) t -> p c t e", e=2),
+                        b_bank[:].rearrange("p t (c e) -> p c t e", e=2),
+                        gate[h, a][:, :, cols].rearrange("p t (c e) -> p c t e", e=2),
+                        MULT,
+                    )
+            z_codes = ring.tile([P, R_PASSES * CHUNK], U32, name="z_codes", align_bytes=64)
+            z_scales = ring.tile([P, R_PASSES * CHUNK], U8, name="z_scales", align_bytes=64)
+            quantize(z_codes, z_scales, z_bf[:].rearrange("p a j t -> p (a j t)"))
+            y_bank = psum.tile([P, N // P, CHUNK], F32, name="y_bank", bufs=1)
+            for u in range(N // P):
+                passes = [((wk_w, wk_s), aq[q], a) for a in range(R_PASSES)] + [(woq, (z_codes, z_scales), a) for a in range(R_PASSES)]
+                for step, (weight, moving, a) in enumerate(passes):
+                    n0 = a * N + u * P
+                    mm(y_bank[:, u, :], weight, slice(n0, n0 + P), moving, slice(a * CHUNK, (a + 1) * CHUNK),
+                       start=(step == 0), stop=(step == len(passes) - 1))
+            y_sb = ring.tile([P, N // P, CHUNK], F32, name="y_sb", align_bytes=64)
+            nc.scalar.copy(y_sb[:], y_bank[:])
+            nc.sync.dma_start(out_rows[:, :, q * CHUNK : (q + 1) * CHUNK], y_sb[:])

@@ -43,7 +43,7 @@ def tile_list_aerosol_activation_features_kernel(
             return held([P, width], U32, name + "_codes"), held([P, width], U8, name + "_scales")
 
         def quantize(codes, scales, values):
-            nc.vector.quantize_mx(out=codes[:].bitcast(FP8X4), scales=scales[:], in_=values)
+            nc.vector.quantize_mx(out=codes.bitcast(FP8X4), scales=scales, in_=values)
 
         def mm(acc, lhs, lhs_cols, rhs, rhs_cols, start=True, stop=True):
             nc.tensor.matmul_mx(
@@ -68,7 +68,7 @@ def tile_list_aerosol_activation_features_kernel(
         pw_sb = held([P, PACK], F32, "pw_sb")
         bg_sb = held([P, R_PASSES, PACK], F32, "bg_sb")
         planes = [held([P, T], F32, "plane%d" % i) for i in range(PACK)]
-        wg_raw = [held([P, PACK, PASS], F32, "wg_raw%d" % a) for a in range(R_PASSES)]
+        wg_raw = {1: held([P, PACK, PASS], F32, "wg_raw1")}
         wx_raw = [held([P, PACK, PASS], F32, "wx_raw%d" % a) for a in range(R_PASSES)]
         wo_raw = held([P, R_PASSES, PACK, N], F32, "wo_raw")
         warm = held([P, 2], F32, "warm")
@@ -82,44 +82,57 @@ def tile_list_aerosol_activation_features_kernel(
         wg_rows = wg.rearrange("(p i) r -> p i r", i=PACK)
         wx_rows = wx.rearrange("(p i) r -> p i r", i=PACK)
 
-        nc.sync.dma_start(list1[:], offs)
-        nc.sync.dma_start(list3[:], offs3)
-        nc.sync.dma_start(list2[:], offs2)
-        for q in range(4):
-            nc.scalar.dma_start(tab_s[32 * q : 32 * q + 4, :].bitcast(I32), tab_scales[0, 4 * q : 4 * q + 4, :].bitcast(I32))
-        nc.sync.dma_start(tab_w[:], tab_words[0].rearrange("p t i -> p (t i)").bitcast(I32))
-        nc.sync.dma_start(wa_raw_w[:].bitcast(I32), wa_words[0].bitcast(I32))
-        for q in range(4):
-            nc.scalar.dma_start(wa_raw_s[32 * q : 32 * q + 4, :].bitcast(I32), wa_scales[0, 4 * q : 4 * q + 4, :].bitcast(I32))
-        nc.scalar.dma_start(pw_sb[:], pw.rearrange("(p i) -> p i", i=PACK))
-        nc.scalar.dma_start(bg_sb[:], bg.rearrange("(a p i) -> p a i", p=P, i=PACK))
-        weight_loads = [(wg_raw[a], wg_rows, a) for a in range(R_PASSES)] + [(wx_raw[a], wx_rows, a) for a in range(R_PASSES)]
-        for i in range(PACK):
+        def load_scale_rows(plane, rows):
+            for q in range(4):
+                nc.sync.dma_start(
+                    plane[32 * q : 32 * q + 4, :].bitcast(I32).rearrange("r (a n) -> r a n", a=rows.shape[0]),
+                    rows[:, 4 * q : 4 * q + 4, :].bitcast(I32).rearrange("a r n -> r a n"),
+                )
+
+        def load_weight_half(raw, rows, a):
+            nc.sync.dma_start(raw[a][:], rows[:, :, a * PASS : (a + 1) * PASS])
+
+        def load_plane(i):
             nc.sync.dma_start(planes[i][:], x_rows[:, i, :])
-            raw, rows, a = weight_loads[i]
-            nc.sync.dma_start(raw[:], rows[:, :, a * PASS : (a + 1) * PASS])
+
+        wg_head = [held([P, PACK, PASS // 2], F32, "wg_head%d" % s) for s in range(2)]
+        nc.sync.dma_start(list1[:], offs)
+        nc.sync.dma_start(pw_sb[:], pw.rearrange("(p i) -> p i", i=PACK))
+        nc.sync.dma_start(wg_head[0][:], wg_rows[:, :, 0 : PASS // 2])
+        nc.sync.dma_start(list3[:], offs3)
+        load_scale_rows(tab_s, tab_scales)
+        nc.sync.dma_start(tab_w[:], tab_words[0].rearrange("p t i -> p (t i)").bitcast(I32))
+        nc.sync.dma_start(wg_head[1][:], wg_rows[:, :, PASS // 2 : PASS])
+        nc.sync.dma_start(wa_raw_w[:].bitcast(I32), wa_words[0].bitcast(I32))
+        nc.sync.dma_start(list2[:], offs2)
+        load_scale_rows(wa_raw_s, wa_scales)
+        load_plane(0)
+        nc.sync.dma_start(bg_sb[:], bg.rearrange("(a p i) -> p a i", p=P, i=PACK))
+        load_weight_half(wg_raw, wg_rows, 1)
+        load_plane(1)
+        load_weight_half(wx_raw, wx_rows, 0)
+        load_plane(2)
+        load_weight_half(wx_raw, wx_rows, 1)
         nc.sync.dma_start(
             wo_raw[:].rearrange("p a i n -> p a (i n)"), wo.rearrange("(a p i) n -> p a (i n)", p=P, i=PACK)
         )
+        load_plane(3)
         nc.sync.dma_start(
             wk_w[:].rearrange("p (a n) -> p a n", a=R_PASSES),
             wk_words.rearrange("a p n i -> p a (n i)").bitcast(I32),
         )
-        for q in range(4):
-            nc.sync.dma_start(
-                wk_s[32 * q : 32 * q + 4, :].bitcast(I32).rearrange("r (a n) -> r a n", a=R_PASSES),
-                wk_scales[:, 4 * q : 4 * q + 4, :].bitcast(I32).rearrange("a r n -> r a n"),
-            )
+        load_scale_rows(wk_s, wk_scales)
 
         def list_half(tile, h):
             return tile[:, h * LIST_COLS : (h + 1) * LIST_COLS]
 
         v = [mx_tiles(HALF, "v%d" % h) for h in range(HALVES)]
-        for h in range(HALVES):
-            nc.vector.tensor_copy(v[h][1][:], tab_s[:].indirect(list_half(list1, h)))
         wa_w = held([P, 2 * H], U8, "wa_w")
         wa_s = held([P, H], U8, "wa_s")
-        nc.vector.tensor_copy(v[0][0][:], tab_w[:].bitcast(U32).indirect(list_half(list1, 0)))
+        for h in range(HALVES):
+            nc.vector.tensor_copy(v[h][1][:], tab_s[:].indirect(list_half(list1, h)))
+        for h in range(HALVES):
+            nc.vector.tensor_copy(v[h][0][:], tab_w[:].bitcast(U32).indirect(list_half(list1, h)))
         nc.vector.tensor_copy(
             wa_w[:].bitcast(U16).rearrange("p (a t m) -> p a m t", a=R_PASSES, t=PACK),
             wa_raw_w[:].bitcast(U16).rearrange("p (a m t) -> p a m t", a=R_PASSES, t=PACK),
@@ -128,64 +141,66 @@ def tile_list_aerosol_activation_features_kernel(
             wa_s[:].rearrange("p (a t m) -> p a m t", a=R_PASSES, t=PACK),
             wa_raw_s[:].rearrange("p (a m t) -> p a m t", a=R_PASSES, t=PACK),
         )
-        nc.vector.tensor_copy(v[1][0][:], tab_w[:].bitcast(U32).indirect(list_half(list1, 1)))
 
-        prod = [held([P, PACK, HALF], F32, "prod%d" % h) for h in range(HALVES)]
-        for i in range(PACK):
-            humid = []
-            for h in range(HALVES):
-                picked = ring.tile([P, HALF], F32, name="picked", bufs=4, align_bytes=64)
-                nc.vector.tensor_copy(picked[:], planes[i][:].indirect(list_half(list3, h)))
-                nc.scalar.activation(picked[:], picked[:], ACT.Copy, scale=pw_sb[:, i : i + 1])
-                humid.append(picked)
-            for h in range(HALVES):
-                nc.vector.tensor_tensor(prod[h][:, i, :], planes[i][:].indirect(list_half(list2, h)), humid[h][:], MULT)
-        xq = [mx_tiles(HALF, "x%d" % h) for h in range(HALVES)]
-        for h in range(HALVES):
-            x_bf = ring.tile([P, HALF * PACK], BF16, name="x_bf", align_bytes=64)
-            nc.vector.tensor_copy(
-                x_bf[:].rearrange("p (c e i) -> p c i e", e=4, i=PACK),
-                prod[h][:].rearrange("p i (c e) -> p c i e", e=4),
-            )
-            quantize(xq[h][0], xq[h][1], x_bf[:])
+        pw_rows = held([P, PACK, HALF], F32, "pw_rows")
+        nc.scalar.copy(pw_rows[:], pw_sb[:].unsqueeze(2).to_broadcast([P, PACK, HALF]))
 
-        def first_stage_weight(raw, name):
-            w_bf = ring.tile([P, PASS * PACK], BF16, name="w_bf", align_bytes=64)
-            nc.scalar.copy(
-                w_bf[:].rearrange("p (u e m i) -> p u m i e", u=2, e=2, i=PACK),
-                raw[:].rearrange("p i (m u e) -> p u m i e", u=2, e=2),
-            )
+        def first_stage_weight(pieces, name):
+            w_bf = held([P, PASS * PACK], BF16, name + "_bf")
+            width = P // len(pieces)
+            for s, raw in enumerate(pieces):
+                nc.scalar.copy(
+                    w_bf[:].rearrange("p (u e m i) -> p u m i e", u=2, e=2, i=PACK)[:, :, s * width : (s + 1) * width],
+                    raw[:].rearrange("p i (m u e) -> p u m i e", u=2, e=2),
+                )
             tiles = mx_tiles(PASS, name)
-            quantize(tiles[0], tiles[1], w_bf[:])
-            return tiles
+            quantize(tiles[0][:], tiles[1][:], w_bf[:])
+            return tiles, w_bf
 
-        wgq = [first_stage_weight(wg_raw[a], "wg%d" % a) for a in range(R_PASSES)]
-        wxq = [first_stage_weight(wx_raw[a], "wx%d" % a) for a in range(R_PASSES)]
-        wo_bf = ring.tile([P, PASS * PACK], BF16, name="w_bf", align_bytes=64)
+        wgq, wg_bf = zip(first_stage_weight(wg_head, "wg0"), first_stage_weight([wg_raw[1]], "wg1"))
+        wxq, wx_bf = zip(*[first_stage_weight([wx_raw[a]], "wx%d" % a) for a in range(R_PASSES)])
+        wo_bf = held([P, PASS * PACK], BF16, "wo_bf")
         nc.scalar.copy(
             wo_bf[:].rearrange("p (a c e i) -> p a c i e", a=R_PASSES, e=2, i=PACK),
             wo_raw[:].rearrange("p a i (c e) -> p a c i e", e=2),
         )
         woq = mx_tiles(R_PASSES * N, "wo")
-        quantize(woq[0], woq[1], wo_bf[:])
+        quantize(woq[0][:], woq[1][:], wo_bf[:])
+
+        prod = [held([P, PACK, HALF], F32, "prod%d" % h) for h in range(HALVES)]
+        xq = [mx_tiles(CHUNK, "x%d" % q) for q in range(CHUNKS)]
+        for i in range(PACK):
+            humid = [ring.tile([P, HALF], F32, name="humid", bufs=4, align_bytes=64) for h in range(HALVES)]
+            for h in range(HALVES):
+                nc.vector.tensor_tensor(humid[h][:], planes[i][:].indirect(list_half(list3, h)), pw_rows[:, i, :], MULT)
+            for h in range(HALVES):
+                nc.vector.tensor_tensor(prod[h][:, i, :], planes[i][:].indirect(list_half(list2, h)), humid[h][:], MULT)
+        for q in range(CHUNKS):
+            h, first = divmod(q * CHUNK, HALF)
+            x_bf = wg_bf[h][:, first * PACK : (first + CHUNK) * PACK]
+            nc.scalar.copy(
+                x_bf.rearrange("p (c e i) -> p c i e", e=2, i=PACK),
+                prod[h][:, :, first : first + CHUNK].rearrange("p i (c e) -> p c i e", e=2),
+            )
+            quantize(xq[q][0][:], xq[q][1][:], x_bf)
 
         gate = {}
         for h in range(HALVES):
             for a in range(R_PASSES):
                 gate[h, a] = held([P, PACK, HALF], F32, "gate%d%d" % (h, a))
                 for t in range(PACK):
-                    c_bank = psum.tile([P, HALF], F32, name="c_bank")
+                    c_bank = psum.tile([P, HALF], F32, name="c_bank", tag="memory", bufs=3)
                     mm(c_bank[:], wgq[a], slice(t * P, (t + 1) * P), v[h], slice(0, HALF))
                     nc.scalar.activation(gate[h, a][:, t, :], c_bank[:], ACT.Sigmoid, bias=bg_sb[:, a, t : t + 1])
 
         aq = [mx_tiles(R_PASSES * CHUNK, "a%d" % q) for q in range(CHUNKS)]
         for q in range(CHUNKS):
             h, first = divmod(q * CHUNK, HALF)
-            a_bf = ring.tile([P, R_PASSES, CHUNK, PACK], BF16, name="a_bf", bufs=3, align_bytes=64)
+            a_bf = held([P, R_PASSES, CHUNK, PACK], BF16, "a_bf%d" % q)
             for a in range(R_PASSES):
                 for j0 in range(0, CHUNK, P):
                     cols = slice(first + j0, first + j0 + P)
-                    a_bank = psum.tile([P, PACK, P], F32, name="a_bank")
+                    a_bank = psum.tile([P, PACK, P], F32, name="a_bank", tag="memory", bufs=3)
                     for t in range(PACK):
                         r0 = a * PASS + t * P
                         nc.tensor.matmul_mx(
@@ -198,34 +213,51 @@ def tile_list_aerosol_activation_features_kernel(
                             stop=True,
                         )
                     nc.scalar.activation(a_bf[:, a, j0 : j0 + P, :], a_bank[:].rearrange("p t j -> p j t"), ACT.Relu)
-            quantize(aq[q][0], aq[q][1], a_bf[:].rearrange("p a j t -> p (a j t)"))
+            quantize(aq[q][0][:], aq[q][1][:], a_bf[:].rearrange("p a j t -> p (a j t)"))
 
         out_rows = out.rearrange("(u p) j -> p u j", p=P)
-        for q in range(CHUNKS):
+        z_room = [wx_bf[0], wx_bf[1], wo_bf, wg_bf[0]]
+        zq = {}
+
+        def gated_bank(q, a, j0):
             h, first = divmod(q * CHUNK, HALF)
-            z_bf = ring.tile([P, R_PASSES, CHUNK, PACK], BF16, name="z_bf", align_bytes=64)
-            for a in range(R_PASSES):
-                for j0 in range(0, CHUNK, P):
-                    cols = slice(first + j0, first + j0 + P)
-                    b_bank = psum.tile([P, PACK, P], F32, name="b_bank", bufs=3)
-                    for t in range(PACK):
-                        mm(b_bank[:, t, :], wxq[a], slice(t * P, (t + 1) * P), xq[h], cols)
-                    nc.vector.tensor_tensor(
-                        z_bf[:, a, j0 : j0 + P, :].rearrange("p (c e) t -> p c t e", e=2),
-                        b_bank[:].rearrange("p t (c e) -> p c t e", e=2),
-                        gate[h, a][:, :, cols].rearrange("p t (c e) -> p c t e", e=2),
-                        MULT,
-                    )
-            z_codes = ring.tile([P, R_PASSES * CHUNK], U32, name="z_codes", align_bytes=64)
-            z_scales = ring.tile([P, R_PASSES * CHUNK], U8, name="z_scales", align_bytes=64)
-            quantize(z_codes, z_scales, z_bf[:].rearrange("p a j t -> p (a j t)"))
-            y_bank = psum.tile([P, N // P, CHUNK], F32, name="y_bank", bufs=1)
-            for u in range(N // P):
-                passes = [((wk_w, wk_s), aq[q], a) for a in range(R_PASSES)] + [(woq, (z_codes, z_scales), a) for a in range(R_PASSES)]
-                for step, (weight, moving, a) in enumerate(passes):
-                    n0 = a * N + u * P
-                    mm(y_bank[:, u, :], weight, slice(n0, n0 + P), moving, slice(a * CHUNK, (a + 1) * CHUNK),
-                       start=(step == 0), stop=(step == len(passes) - 1))
+            b_bank = psum.tile([P, PACK, P], F32, name="b_bank", bufs=3)
+            for t in range(PACK):
+                mm(b_bank[:, t, :], wxq[a], slice(t * P, (t + 1) * P), xq[q], slice(j0, j0 + P))
+            at = (a * CHUNK + j0) * PACK
+            nc.vector.tensor_tensor(
+                z_room[q][:, at : at + P * PACK].rearrange("p (c e t) -> p c t e", e=2, t=PACK),
+                b_bank[:].rearrange("p t (c e) -> p c t e", e=2),
+                gate[h, a][:, :, first + j0 : first + j0 + P].rearrange("p t (c e) -> p c t e", e=2),
+                MULT,
+            )
+
+        def finish(q, a):
+            if a == 0:
+                zq[q] = (
+                    ring.tile([P, R_PASSES * CHUNK], U32, name="z_codes", align_bytes=64),
+                    ring.tile([P, R_PASSES * CHUNK], U8, name="z_scales", align_bytes=64),
+                )
+            cols = slice(a * CHUNK, (a + 1) * CHUNK)
+            quantize(zq[q][0][:, cols], zq[q][1][:, cols], z_room[q][:, a * CHUNK * PACK : (a + 1) * CHUNK * PACK])
+            if a < R_PASSES - 1:
+                return
             y_sb = ring.tile([P, N // P, CHUNK], F32, name="y_sb", align_bytes=64)
-            nc.scalar.copy(y_sb[:], y_bank[:])
+            y_banks = [psum.tile([P, CHUNK], F32, name="y_bank") for u in range(N // P)]
+            passes = [((wk_w, wk_s), aq[q], r) for r in range(R_PASSES)] + [(woq, zq[q], r) for r in range(R_PASSES)]
+            for step, (weight, moving, r) in enumerate(passes):
+                for u in range(N // P):
+                    n0 = r * N + u * P
+                    mm(y_banks[u][:], weight, slice(n0, n0 + P), moving, slice(r * CHUNK, (r + 1) * CHUNK),
+                       start=(step == 0), stop=(step == len(passes) - 1))
+            for u in range(N // P):
+                nc.scalar.copy(y_sb[:, u, :], y_banks[u][:])
             nc.sync.dma_start(out_rows[:, :, q * CHUNK : (q + 1) * CHUNK], y_sb[:])
+
+        steps = [(q, a) for q in range(CHUNKS) for a in range(R_PASSES)]
+        for n, (q, a) in enumerate(steps):
+            gated_bank(q, a, 0)
+            if n > 0:
+                finish(*steps[n - 1])
+            gated_bank(q, a, P)
+        finish(*steps[-1])

@@ -134,12 +134,12 @@ def tile_list_aerosol_activation_features_kernel(
         for h in range(HALVES):
             nc.vector.tensor_copy(v[h][0][:], tab_w[:].bitcast(U32).indirect(list_half(list1, h)))
         nc.vector.tensor_copy(
-            wa_w[:].bitcast(U16).rearrange("p (a t m) -> p a m t", a=R_PASSES, t=PACK),
-            wa_raw_w[:].bitcast(U16).rearrange("p (a m t) -> p a m t", a=R_PASSES, t=PACK),
+            wa_w[:].bitcast(U16).rearrange("p (a t m) -> p a t m", a=R_PASSES, t=PACK),
+            wa_raw_w[:].bitcast(U16).rearrange("p (a m t) -> p a t m", a=R_PASSES, t=PACK),
         )
         nc.vector.tensor_copy(
-            wa_s[:].rearrange("p (a t m) -> p a m t", a=R_PASSES, t=PACK),
-            wa_raw_s[:].rearrange("p (a m t) -> p a m t", a=R_PASSES, t=PACK),
+            wa_s[:].rearrange("p (a t m) -> p a t m", a=R_PASSES, t=PACK),
+            wa_raw_s[:].rearrange("p (a m t) -> p a t m", a=R_PASSES, t=PACK),
         )
 
         pw_rows = held([P, PACK, HALF], F32, "pw_rows")
@@ -170,12 +170,22 @@ def tile_list_aerosol_activation_features_kernel(
         prod = [held([P, PACK, HALF], F32, "prod%d" % h) for h in range(HALVES)]
         xq = [mx_tiles(CHUNK, "x%d" % q) for q in range(CHUNKS)]
         for i in range(PACK):
-            humid = [ring.tile([P, HALF], F32, name="humid", bufs=4, align_bytes=64) for h in range(HALVES)]
-            for h in range(HALVES):
-                nc.vector.tensor_tensor(humid[h][:], planes[i][:].indirect(list_half(list3, h)), pw_rows[:, i, :], MULT)
-            for h in range(HALVES):
-                nc.vector.tensor_tensor(prod[h][:, i, :], planes[i][:].indirect(list_half(list2, h)), humid[h][:], MULT)
-        for q in range(CHUNKS):
+            width = HALF if i < PACK - 1 else CHUNK
+            for pair in range(0, S, 2 * width):
+                starts = (pair, pair + width)
+                humid = [ring.tile([P, width], F32, name="humid", bufs=4, align_bytes=64) for j in starts]
+                for j, picked in zip(starts, humid):
+                    nc.vector.tensor_tensor(
+                        picked[:], planes[i][:].indirect(list3[:, j // 16 : (j + width) // 16]), pw_rows[:, i, :width], MULT
+                    )
+                for j, picked in zip(starts, humid):
+                    nc.vector.tensor_tensor(
+                        prod[j // HALF][:, i, j % HALF : j % HALF + width],
+                        planes[i][:].indirect(list2[:, j // 16 : (j + width) // 16]),
+                        picked[:],
+                        MULT,
+                    )
+        def weather_operand(q):
             h, first = divmod(q * CHUNK, HALF)
             x_bf = wg_bf[h][:, first * PACK : (first + CHUNK) * PACK]
             nc.scalar.copy(
@@ -185,22 +195,23 @@ def tile_list_aerosol_activation_features_kernel(
             quantize(xq[q][0][:], xq[q][1][:], x_bf)
 
         gate = {}
-        for h in range(HALVES):
-            for a in range(R_PASSES):
-                gate[h, a] = held([P, PACK, HALF], F32, "gate%d%d" % (h, a))
-                for t in range(PACK):
-                    c_bank = psum.tile([P, HALF], F32, name="c_bank", tag="memory", bufs=3)
-                    mm(c_bank[:], wgq[a], slice(t * P, (t + 1) * P), v[h], slice(0, HALF))
-                    nc.scalar.activation(gate[h, a][:, t, :], c_bank[:], ACT.Sigmoid, bias=bg_sb[:, a, t : t + 1])
+
+        def gate_rows(h, a):
+            gate[h, a] = held([P, PACK, HALF], F32, "gate%d%d" % (h, a))
+            for t in range(PACK):
+                c_bank = psum.tile([P, HALF], F32, name="c_bank", tag="memory", bufs=4)
+                mm(c_bank[:], wgq[a], slice(t * P, (t + 1) * P), v[h], slice(0, HALF))
+                nc.scalar.activation(gate[h, a][:, t, :], c_bank[:], ACT.Sigmoid, bias=bg_sb[:, a, t : t + 1])
 
         aq = [mx_tiles(R_PASSES * CHUNK, "a%d" % q) for q in range(CHUNKS)]
-        for q in range(CHUNKS):
+
+        def memory_operand(q):
             h, first = divmod(q * CHUNK, HALF)
             a_bf = held([P, R_PASSES, CHUNK, PACK], BF16, "a_bf%d" % q)
             for a in range(R_PASSES):
                 for j0 in range(0, CHUNK, P):
                     cols = slice(first + j0, first + j0 + P)
-                    a_bank = psum.tile([P, PACK, P], F32, name="a_bank", tag="memory", bufs=3)
+                    a_bank = psum.tile([P, PACK, P], F32, name="a_bank", tag="memory", bufs=4)
                     for t in range(PACK):
                         r0 = a * PASS + t * P
                         nc.tensor.matmul_mx(
@@ -215,13 +226,27 @@ def tile_list_aerosol_activation_features_kernel(
                     nc.scalar.activation(a_bf[:, a, j0 : j0 + P, :], a_bank[:].rearrange("p t j -> p j t"), ACT.Relu)
             quantize(aq[q][0][:], aq[q][1][:], a_bf[:].rearrange("p a j t -> p (a j t)"))
 
+
+        gate_rows(0, 0)
+        gate_rows(1, 0)
+        memory_operand(0)
+        memory_operand(1)
+        gate_rows(0, 1)
+        weather_operand(0)
+        weather_operand(1)
+        gate_rows(1, 1)
+        weather_operand(2)
+        weather_operand(3)
+        memory_operand(2)
+        memory_operand(3)
+
         out_rows = out.rearrange("(u p) j -> p u j", p=P)
         z_room = [wx_bf[0], wx_bf[1], wo_bf, wg_bf[0]]
         zq = {}
 
         def gated_bank(q, a, j0):
             h, first = divmod(q * CHUNK, HALF)
-            b_bank = psum.tile([P, PACK, P], F32, name="b_bank", bufs=3)
+            b_bank = psum.tile([P, PACK, P], F32, name="b_bank", bufs=4)
             for t in range(PACK):
                 mm(b_bank[:, t, :], wxq[a], slice(t * P, (t + 1) * P), xq[q], slice(j0, j0 + P))
             at = (a * CHUNK + j0) * PACK
@@ -232,32 +257,43 @@ def tile_list_aerosol_activation_features_kernel(
                 MULT,
             )
 
-        def finish(q, a):
+        def finish(j, width, a):
+            q, first = divmod(j, CHUNK)
             if a == 0:
-                zq[q] = (
-                    ring.tile([P, R_PASSES * CHUNK], U32, name="z_codes", align_bytes=64),
-                    ring.tile([P, R_PASSES * CHUNK], U8, name="z_scales", align_bytes=64),
+                zq[j] = (
+                    ring.tile([P, R_PASSES * width], U32, name="z_codes", align_bytes=64),
+                    ring.tile([P, R_PASSES * width], U8, name="z_scales", align_bytes=64),
                 )
-            cols = slice(a * CHUNK, (a + 1) * CHUNK)
-            quantize(zq[q][0][:, cols], zq[q][1][:, cols], z_room[q][:, a * CHUNK * PACK : (a + 1) * CHUNK * PACK])
+            cols = slice(a * width, (a + 1) * width)
+            at = (a * CHUNK + first) * PACK
+            quantize(zq[j][0][:, cols], zq[j][1][:, cols], z_room[q][:, at : at + width * PACK])
             if a < R_PASSES - 1:
                 return
-            y_sb = ring.tile([P, N // P, CHUNK], F32, name="y_sb", align_bytes=64)
-            y_banks = [psum.tile([P, CHUNK], F32, name="y_bank") for u in range(N // P)]
-            passes = [((wk_w, wk_s), aq[q], r) for r in range(R_PASSES)] + [(woq, zq[q], r) for r in range(R_PASSES)]
-            for step, (weight, moving, r) in enumerate(passes):
+            y_banks = [psum.tile([P, width], F32, name="y_bank", tag="memory", bufs=4) for u in range(N // P)]
+            gated = [(woq, r, zq[j], r * width) for r in range(R_PASSES)]
+            skip = [((wk_w, wk_s), r, aq[q], r * CHUNK + first) for r in range(R_PASSES)]
+            passes = gated[:1] + skip + gated[1:]
+            for step, (weight, r, moving, c0) in enumerate(passes):
                 for u in range(N // P):
                     n0 = r * N + u * P
-                    mm(y_banks[u][:], weight, slice(n0, n0 + P), moving, slice(r * CHUNK, (r + 1) * CHUNK),
+                    mm(y_banks[u][:], weight, slice(n0, n0 + P), moving, slice(c0, c0 + width),
                        start=(step == 0), stop=(step == len(passes) - 1))
-            for u in range(N // P):
-                nc.scalar.copy(y_sb[:, u, :], y_banks[u][:])
-            nc.sync.dma_start(out_rows[:, :, q * CHUNK : (q + 1) * CHUNK], y_sb[:])
+            y_sb = ring.tile([P, N // P, width], F32, name="y_sb", align_bytes=64)
+            nc.scalar.copy(y_sb[:, 0, :], y_banks[0][:])
+            if j + width < S:
+                nc.scalar.copy(y_sb[:, 1, :], y_banks[1][:])
+            else:
+                nc.vector.tensor_copy(y_sb[:, 1, :], y_banks[1][:])
+            nc.sync.dma_start(out_rows[:, :, j : j + width], y_sb[:])
 
-        steps = [(q, a) for q in range(CHUNKS) for a in range(R_PASSES)]
-        for n, (q, a) in enumerate(steps):
-            gated_bank(q, a, 0)
-            if n > 0:
-                finish(*steps[n - 1])
-            gated_bank(q, a, P)
-        finish(*steps[-1])
+        pieces = [(j, CHUNK) for j in range(0, S - CHUNK, CHUNK)] + [(j, P) for j in range(S - CHUNK, S, P)]
+        waiting = None
+        for j, width in pieces:
+            for a in range(R_PASSES):
+                for j0 in range(j, j + width, P):
+                    gated_bank(j0 // CHUNK, a, j0 % CHUNK)
+                    if waiting is not None:
+                        finish(*waiting)
+                        waiting = None
+                waiting = (j, width, a)
+        finish(*waiting)

from contextlib import ExitStack

import concourse.mybir as mybir

K, H, N, T, S = 512, 1024, 256, 2048, 1024
FLOPS = 2 * S * (3 * K * H + 2 * H * N)

F32 = mybir.dt.float32
BF16 = mybir.dt.bfloat16
I32 = mybir.dt.int32
U32 = mybir.dt.uint32
U16 = mybir.dt.uint16
U8 = mybir.dt.uint8
FP8X4 = mybir.dt.float8_e4m3fn_x4
FP4X4 = mybir.dt.float4_e2m1fn_x4
ACT = mybir.ActivationFunctionType
MULT = mybir.AluOpType.mult

P = 128
PACK = 4
PASS = P * PACK
R_PASSES = H // PASS
HALF = 512
HALVES = S // HALF
CHUNK = 256
CHUNKS = S // CHUNK
LIST_COLS = HALF // 16


def tile_list_aerosol_activation_features_kernel(
    tc, tab_words, tab_scales, offs, xT, offs2, offs3, pw, wa_words, wa_scales, wg, bg, wx, wo, wk_words, wk_scales, out
):
    nc = tc.nc
    with ExitStack() as ctx:
        keep = ctx.enter_context(tc.tile_pool(name="keep", bufs=1))
        ring = ctx.enter_context(tc.tile_pool(name="ring", bufs=2))
        psum = ctx.enter_context(tc.psum_pool(name="psum", bufs=2))

        def held(shape, dtype, name):
            return keep.tile(shape, dtype, name=name, align_bytes=64)

        def mx_tiles(width, name):
            return held([P, width], U32, name + "_codes"), held([P, width], U8, name + "_scales")

        def quantize(codes, scales, values):
            nc.vector.quantize_mx(out=codes.bitcast(FP8X4), scales=scales, in_=values)

        def mm(acc, lhs, lhs_cols, rhs, rhs_cols, start=True, stop=True):
            nc.tensor.matmul_mx(
                out=acc,
                lhsT=lhs[0][:, lhs_cols].bitcast(FP8X4),
                lhsT_scale=lhs[1][:, lhs_cols],
                rhs=rhs[0][:, rhs_cols].bitcast(FP8X4),
                rhs_scale=rhs[1][:, rhs_cols],
                start=start,
                stop=stop,
            )

        list1 = held([P, S // 16], U16, "list1")
        list2 = held([P, S // 16], U16, "list2")
        list3 = held([P, S // 16], U16, "list3")
        tab_w = held([P, T], I32, "tab_w")
        tab_s = held([P, T], U8, "tab_s")
        wa_raw_w = held([P, 2 * H], U8, "wa_raw_w")
        wa_raw_s = held([P, H], U8, "wa_raw_s")
        wk_w = held([P, R_PASSES * N], I32, "wk_w")
        wk_s = held([P, R_PASSES * N], U8, "wk_s")
        pw_sb = held([P, PACK], F32, "pw_sb")
        bg_sb = held([P, R_PASSES, PACK], F32, "bg_sb")
        planes = [held([P, T], F32, "plane%d" % i) for i in range(PACK)]
        wg_raw = {1: held([P, PACK, PASS], F32, "wg_raw1")}
        wx_raw = [held([P, PACK, PASS], F32, "wx_raw%d" % a) for a in range(R_PASSES)]
        wo_raw = held([P, R_PASSES, PACK, N], F32, "wo_raw")
        warm = held([P, 2], F32, "warm")

        for plane in (tab_s, wa_raw_s, wk_s):
            nc.gpsimd.memset(plane[:].bitcast(I32), 0)
        nc.vector.memset(warm[:, 0:1], 0.0)
        nc.scalar.activation(warm[:, 1:2], warm[:, 0:1], ACT.Sigmoid)

        x_rows = xT.rearrange("(p i) t -> p i t", i=PACK)
        wg_rows = wg.rearrange("(p i) r -> p i r", i=PACK)
        wx_rows = wx.rearrange("(p i) r -> p i r", i=PACK)

        def load_scale_rows(plane, rows):
            for q in range(4):
                nc.sync.dma_start(
                    plane[32 * q : 32 * q + 4, :].bitcast(I32).rearrange("r (a n) -> r a n", a=rows.shape[0]),
                    rows[:, 4 * q : 4 * q + 4, :].bitcast(I32).rearrange("a r n -> r a n"),
                )

        def load_weight_half(raw, rows, a):
            nc.sync.dma_start(raw[a][:], rows[:, :, a * PASS : (a + 1) * PASS])

        def load_plane(i):
            nc.sync.dma_start(planes[i][:], x_rows[:, i, :])

        wg_head = [held([P, PACK, PASS // 2], F32, "wg_head%d" % s) for s in range(2)]
        nc.sync.dma_start(list1[:], offs)
        nc.sync.dma_start(pw_sb[:], pw.rearrange("(p i) -> p i", i=PACK))
        nc.sync.dma_start(wg_head[0][:], wg_rows[:, :, 0 : PASS // 2])
        nc.sync.dma_start(list3[:], offs3)
        load_scale_rows(tab_s, tab_scales)
        nc.sync.dma_start(tab_w[:], tab_words[0].rearrange("p t i -> p (t i)").bitcast(I32))
        nc.sync.dma_start(wg_head[1][:], wg_rows[:, :, PASS // 2 : PASS])
        nc.sync.dma_start(wa_raw_w[:].bitcast(I32), wa_words[0].bitcast(I32))
        nc.sync.dma_start(list2[:], offs2)
        load_scale_rows(wa_raw_s, wa_scales)
        load_plane(0)
        nc.sync.dma_start(bg_sb[:], bg.rearrange("(a p i) -> p a i", p=P, i=PACK))
        load_weight_half(wg_raw, wg_rows, 1)
        load_plane(1)
        load_weight_half(wx_raw, wx_rows, 0)
        load_plane(2)
        load_weight_half(wx_raw, wx_rows, 1)
        nc.sync.dma_start(
            wo_raw[:].rearrange("p a i n -> p a (i n)"), wo.rearrange("(a p i) n -> p a (i n)", p=P, i=PACK)
        )
        load_plane(3)
        nc.sync.dma_start(
            wk_w[:].rearrange("p (a n) -> p a n", a=R_PASSES),
            wk_words.rearrange("a p n i -> p a (n i)").bitcast(I32),
        )
        load_scale_rows(wk_s, wk_scales)

        def list_half(tile, h):
            return tile[:, h * LIST_COLS : (h + 1) * LIST_COLS]

        v = [mx_tiles(HALF, "v%d" % h) for h in range(HALVES)]
        wa_w = held([P, 2 * H], U8, "wa_w")
        wa_s = held([P, H], U8, "wa_s")
        for h in range(HALVES):
            nc.vector.tensor_copy(v[h][1][:], tab_s[:].indirect(list_half(list1, h)))
        for h in range(HALVES):
            nc.vector.tensor_copy(v[h][0][:], tab_w[:].bitcast(U32).indirect(list_half(list1, h)))
        nc.vector.tensor_copy(
            wa_w[:].bitcast(U16).rearrange("p (a t m) -> p a t m", a=R_PASSES, t=PACK),
            wa_raw_w[:].bitcast(U16).rearrange("p (a m t) -> p a t m", a=R_PASSES, t=PACK),
        )
        nc.vector.tensor_copy(
            wa_s[:].rearrange("p (a t m) -> p a t m", a=R_PASSES, t=PACK),
            wa_raw_s[:].rearrange("p (a m t) -> p a t m", a=R_PASSES, t=PACK),
        )

        pw_rows = held([P, PACK, HALF], F32, "pw_rows")
        nc.scalar.copy(pw_rows[:], pw_sb[:].unsqueeze(2).to_broadcast([P, PACK, HALF]))

        def first_stage_weight(pieces, name):
            w_bf = held([P, PASS * PACK], BF16, name + "_bf")
            width = P // len(pieces)
            for s, raw in enumerate(pieces):
                nc.scalar.copy(
                    w_bf[:].rearrange("p (u e m i) -> p u m i e", u=2, e=2, i=PACK)[:, :, s * width : (s + 1) * width],
                    raw[:].rearrange("p i (m u e) -> p u m i e", u=2, e=2),
                )
            tiles = mx_tiles(PASS, name)
            quantize(tiles[0][:], tiles[1][:], w_bf[:])
            return tiles, w_bf

        wgq, wg_bf = zip(first_stage_weight(wg_head, "wg0"), first_stage_weight([wg_raw[1]], "wg1"))
        wxq, wx_bf = zip(*[first_stage_weight([wx_raw[a]], "wx%d" % a) for a in range(R_PASSES)])
        wo_bf = held([P, PASS * PACK], BF16, "wo_bf")
        nc.scalar.copy(
            wo_bf[:].rearrange("p (a c e i) -> p a c i e", a=R_PASSES, e=2, i=PACK),
            wo_raw[:].rearrange("p a i (c e) -> p a c i e", e=2),
        )
        woq = mx_tiles(R_PASSES * N, "wo")
        quantize(woq[0][:], woq[1][:], wo_bf[:])

        prod = [held([P, PACK, HALF], F32, "prod%d" % h) for h in range(HALVES)]
        xq = [mx_tiles(CHUNK, "x%d" % q) for q in range(CHUNKS)]
        for i in range(PACK):
            width = HALF if i < PACK - 1 else CHUNK
            for pair in range(0, S, 2 * width):
                starts = (pair, pair + width)
                humid = [ring.tile([P, width], F32, name="humid", bufs=4, align_bytes=64) for j in starts]
                for j, picked in zip(starts, humid):
                    nc.vector.tensor_tensor(
                        picked[:], planes[i][:].indirect(list3[:, j // 16 : (j + width) // 16]), pw_rows[:, i, :width], MULT
                    )
                for j, picked in zip(starts, humid):
                    nc.vector.tensor_tensor(
                        prod[j // HALF][:, i, j % HALF : j % HALF + width],
                        planes[i][:].indirect(list2[:, j // 16 : (j + width) // 16]),
                        picked[:],
                        MULT,
                    )
        def weather_operand(q):
            h, first = divmod(q * CHUNK, HALF)
            x_bf = wg_bf[h][:, first * PACK : (first + CHUNK) * PACK]
            nc.scalar.copy(
                x_bf.rearrange("p (c e i) -> p c i e", e=2, i=PACK),
                prod[h][:, :, first : first + CHUNK].rearrange("p i (c e) -> p c i e", e=2),
            )
            quantize(xq[q][0][:], xq[q][1][:], x_bf)

        gate = {}

        def gate_rows(h, a):
            gate[h, a] = held([P, PACK, HALF], F32, "gate%d%d" % (h, a))
            for t in range(PACK):
                c_bank = psum.tile([P, HALF], F32, name="c_bank", tag="memory", bufs=4)
                mm(c_bank[:], wgq[a], slice(t * P, (t + 1) * P), v[h], slice(0, HALF))
                nc.scalar.activation(gate[h, a][:, t, :], c_bank[:], ACT.Sigmoid, bias=bg_sb[:, a, t : t + 1])

        aq = [mx_tiles(R_PASSES * CHUNK, "a%d" % q) for q in range(CHUNKS)]

        def memory_operand(q):
            h, first = divmod(q * CHUNK, HALF)
            a_bf = held([P, R_PASSES, CHUNK, PACK], BF16, "a_bf%d" % q)
            for a in range(R_PASSES):
                for j0 in range(0, CHUNK, P):
                    cols = slice(first + j0, first + j0 + P)
                    a_bank = psum.tile([P, PACK, P], F32, name="a_bank", tag="memory", bufs=4)
                    for t in range(PACK):
                        r0 = a * PASS + t * P
                        nc.tensor.matmul_mx(
                            out=a_bank[:, t, :],
                            lhsT=wa_w[:, 2 * r0 : 2 * (r0 + P)].bitcast(FP4X4),
                            lhsT_scale=wa_s[:, r0 : r0 + P],
                            rhs=v[h][0][:, cols].bitcast(FP8X4),
                            rhs_scale=v[h][1][:, cols],
                            start=True,
                            stop=True,
                        )
                    nc.scalar.activation(a_bf[:, a, j0 : j0 + P, :], a_bank[:].rearrange("p t j -> p j t"), ACT.Relu)
            quantize(aq[q][0][:], aq[q][1][:], a_bf[:].rearrange("p a j t -> p (a j t)"))


        gate_rows(0, 0)
        gate_rows(1, 0)
        memory_operand(0)
        memory_operand(1)
        gate_rows(0, 1)
        weather_operand(0)
        weather_operand(1)
        gate_rows(1, 1)
        weather_operand(2)
        weather_operand(3)
        memory_operand(2)
        memory_operand(3)

        out_rows = out.rearrange("(u p) j -> p u j", p=P)
        z_room = [wx_bf[0], wx_bf[1], wo_bf, wg_bf[0]]
        zq = {}

        def gated_bank(q, a, j0):
            h, first = divmod(q * CHUNK, HALF)
            b_bank = psum.tile([P, PACK, P], F32, name="b_bank", bufs=4)
            for t in range(PACK):
                mm(b_bank[:, t, :], wxq[a], slice(t * P, (t + 1) * P), xq[q], slice(j0, j0 + P))
            at = (a * CHUNK + j0) * PACK
            nc.vector.tensor_tensor(
                z_room[q][:, at : at + P * PACK].rearrange("p (c e t) -> p c t e", e=2, t=PACK),
                b_bank[:].rearrange("p t (c e) -> p c t e", e=2),
                gate[h, a][:, :, first + j0 : first + j0 + P].rearrange("p t (c e) -> p c t e", e=2),
                MULT,
            )

        def finish(j, width, a):
            q, first = divmod(j, CHUNK)
            if a == 0:
                zq[j] = (
                    ring.tile([P, R_PASSES * width], U32, name="z_codes", align_bytes=64),
                    ring.tile([P, R_PASSES * width], U8, name="z_scales", align_bytes=64),
                )
            cols = slice(a * width, (a + 1) * width)
            at = (a * CHUNK + first) * PACK
            quantize(zq[j][0][:, cols], zq[j][1][:, cols], z_room[q][:, at : at + width * PACK])
            if a < R_PASSES - 1:
                return
            y_banks = [psum.tile([P, width], F32, name="y_bank", tag="memory", bufs=4) for u in range(N // P)]
            gated = [(woq, r, zq[j], r * width) for r in range(R_PASSES)]
            skip = [((wk_w, wk_s), r, aq[q], r * CHUNK + first) for r in range(R_PASSES)]
            passes = gated[:1] + skip + gated[1:]
            for step, (weight, r, moving, c0) in enumerate(passes):
                for u in range(N // P):
                    n0 = r * N + u * P
                    mm(y_banks[u][:], weight, slice(n0, n0 + P), moving, slice(c0, c0 + width),
                       start=(step == 0), stop=(step == len(passes) - 1))
            y_sb = ring.tile([P, N // P, width], F32, name="y_sb", align_bytes=64)
            nc.scalar.copy(y_sb[:, 0, :], y_banks[0][:])
            if j + width < S:
                nc.scalar.copy(y_sb[:, 1, :], y_banks[1][:])
            else:
                nc.vector.tensor_copy(y_sb[:, 1, :], y_banks[1][:])
            nc.sync.dma_start(out_rows[:, :, j : j + width], y_sb[:])

        pieces = [(j, CHUNK) for j in range(0, S - CHUNK, CHUNK)] + [(j, P) for j in range(S - CHUNK, S, P)]
        waiting = None
        for j, width in pieces:
            for a in range(R_PASSES):
                for j0 in range(j, j + width, P):
                    gated_bank(j0 // CHUNK, a, j0 % CHUNK)
                    if waiting is not None:
                        finish(*waiting)
                        waiting = None
                waiting = (j, width, a)
        finish(*waiting)
